import numpy as np
import ml_dtypes


def mxq(x, axis, fmt="e4m3"):
    dtype, down = {"e4m3": (ml_dtypes.float8_e4m3fn, 7), "e5m2": (ml_dtypes.float8_e5m2, 14)}[fmt]
    v = np.moveaxis(np.asarray(x, np.float32).astype(ml_dtypes.bfloat16).astype(np.float64), axis, -1)
    blocks = v.reshape(v.shape[:-1] + (-1, 32))
    amax = np.abs(blocks).max(-1, keepdims=True)
    byte = np.maximum(np.where(amax > 0, np.frexp(amax)[1] - 1 + 127, 0) - down, 1)
    scale = np.exp2(byte - 127.0)
    codes = (blocks / scale).astype(np.float32).astype(dtype).astype(np.float64)
    return np.moveaxis((codes * scale).reshape(v.shape), -1, axis)


WIDE = False


def mx_kscale(k):
    if not WIDE:
        return np.ones(k)
    levels = np.array([10, -10, 5, -5, 0])
    if k % 512:
        return np.exp2(np.random.permutation(np.resize(levels, k // 32))).repeat(32)
    a = np.empty((k // 512, 16))
    for p in range(k // 512):
        a[p, :8] = np.random.permutation(np.resize(levels, 8))
        for g in range(8):
            far = levels[np.abs(levels - a[p, g]) >= 10]
            a[p, g + 8] = far[np.random.randint(len(far))]
    return np.exp2(a.ravel()).repeat(32)


def f64(x):
    return np.asarray(x).astype(np.float64)


def striped(idx):
    return np.tile(np.asarray(idx).reshape(-1, 16).T, (8, 1)).astype(np.uint16)


def unstriped(offs):
    return offs[:16].T.reshape(-1).astype(np.int64)


E2M1 = np.array([0.0, 0.5, 1.0, 1.5, 2.0, 3.0, 4.0, 6.0, -0.0, -0.5, -1.0, -1.5, -2.0, -3.0, -4.0, -6.0])


def pack_weight(w, fmt):
    k, n = w.shape
    w = f64(np.asarray(w, np.float32).astype(ml_dtypes.bfloat16)).reshape(k // 32, 32, n)
    amax = np.abs(w).max(1)
    if fmt == "e4m3":
        byte = np.frexp(amax)[1] - 1 + 127 - 7
    else:
        mant, ex = np.frexp(amax / 6.0)
        byte = np.where(mant > 0.5, ex, ex - 1) + 127
    byte = np.clip(np.where(amax > 0, byte, 1), 1, 254)
    scaled = (w * np.exp2(127.0 - byte)[:, None, :]).reshape(k, n).astype(np.float32)
    by_word = np.ascontiguousarray(scaled.reshape(k // 512, 128, 4, n).transpose(0, 1, 3, 2))
    if fmt == "e4m3":
        words = by_word.astype(ml_dtypes.float8_e4m3fn).view(np.uint8)
    else:
        c = by_word.astype(ml_dtypes.float4_e2m1fn).view(np.uint8) & 0xF
        words = (c[..., 0::2] | (c[..., 1::2] << 4)).reshape(k // 512, 128, 2 * n)
    return np.ascontiguousarray(words), np.ascontiguousarray(byte.astype(np.uint8).reshape(k // 512, 16, n))


def unpack_weight(words, scales, fmt):
    g, _, n = scales.shape
    words = np.ascontiguousarray(words).reshape(g, 128, n, -1)
    if fmt == "e4m3":
        vals = words.view(ml_dtypes.float8_e4m3fn).astype(np.float64)
    else:
        nib = np.empty((g, 128, n, 4), np.uint8)
        nib[..., 0::2] = words & 0xF
        nib[..., 1::2] = words >> 4
        vals = E2M1[nib]
    vals = vals * np.repeat(np.exp2(scales.astype(np.float64) - 127.0), 8, axis=1)[..., None]
    return vals.transpose(0, 1, 3, 2).reshape(g * 512, n)


B, N, T, D, NQ = 1, 512, 2048, 1024, 128
SEG = 8


def setup_inputs():
    n = np.random.standard_normal
    idx = np.random.permutation(T)[:B * N]
    s = mx_kscale(D)[:, None]
    mid = n((D, T))
    kp = pack_weight((mid + np.abs(n((D, T)))) / s, "e2m1")
    cp = pack_weight((mid - np.abs(n((D, T)))) / s, "e2m1")
    return {
        "qT": (n((B, D, NQ)) * s * (1.00 / np.sqrt(D))).astype(np.float32),
        "k_words": np.ascontiguousarray(kp[0].reshape(1, 2, 128, T, 2).transpose(0, 2, 3, 1, 4)).reshape(1, 128, T, 4),
        "k_scales": kp[1],
        "c_words": np.ascontiguousarray(cp[0].reshape(1, 2, 128, T, 2).transpose(0, 2, 3, 1, 4)).reshape(1, 128, T, 4),
        "c_scales": cp[1],
        "th": (n((B, NQ, 1))).astype(np.float32),
        "offs": striped(idx),
    }


def reference(qT, k_words, k_scales, c_words, c_scales, th, offs):
    idx = unstriped(offs)
    pick = lambda x, which: x[:, which].reshape(x.shape[0], B, -1).transpose(1, 0, 2)
    k = unpack_weight(k_words.reshape(1, 128, T, 2, 2).transpose(0, 3, 1, 2, 4).reshape(2, 128, 2 * T), k_scales, "e2m1")
    kg = pick(k, idx)
    c = unpack_weight(c_words.reshape(1, 128, T, 2, 2).transpose(0, 3, 1, 2, 4).reshape(2, 128, 2 * T), c_scales, "e2m1")
    cg = pick(c, idx)
    hiq = mxq(np.maximum(f64(qT), 0.0), 1, "e4m3")
    loq = mxq(np.minimum(f64(qT), 0.0), 1, "e4m3")
    a = (hiq.transpose(0, 2, 1) @ kg) + (loq.transpose(0, 2, 1) @ cg)
    y = a.reshape(B, NQ, N // SEG, SEG).max(-1) - f64(th)
    return y

@@ -1,0 +1,157 @@
+from contextlib import ExitStack
+
+import concourse.mybir as mybir
+
+N, T, D, NQ, SEG = 512, 2048, 1024, 128, 8
+FLOPS = 2 * 2 * NQ * N * D
+
+F32 = mybir.dt.float32
+BF16 = mybir.dt.bfloat16
+I32 = mybir.dt.int32
+U32 = mybir.dt.uint32
+U16 = mybir.dt.uint16
+U8 = mybir.dt.uint8
+FP8X4 = mybir.dt.float8_e4m3fn_x4
+FP4X4 = mybir.dt.float4_e2m1fn_x4
+ACT = mybir.ActivationFunctionType
+ALU = mybir.AluOpType
+
+P = 128
+PACK = 4
+PASSES = D // (P * PACK)
+GROUP = 128
+GROUPS = N // GROUP
+HALF = N // 2
+
+
+def tile_attend_questgrp_topk_kernel(tc, qT, k_words, k_scales, c_words, c_scales, th, offs, out):
+    nc = tc.nc
+    with ExitStack() as ctx:
+        pool = ctx.enter_context(tc.tile_pool(name="held", bufs=1))
+        psum = ctx.enter_context(tc.psum_pool(name="psum", bufs=1))
+
+        offsets = pool.tile([P, N // 16], U16, name="offsets")
+        nc.sync.dma_start(offsets[:], offs)
+
+        def load_scale_rows(name, scales, row0, empty):
+            rows = pool.tile([P, T], U8, name=name, align_bytes=64)
+            nc.sync.dma_start(
+                out=rows[row0 : row0 + 32, :].bitcast(I32),
+                in_=scales.bitcast(I32).rearrange("o f t -> f o t"),
+            )
+            for a, b in empty:
+                nc.vector.memset(rows[a:b, :].bitcast(I32), 0)
+            return rows
+
+        k_rows = load_scale_rows("k_rows", k_scales, 0, [(32, 64), (64, 128)])
+        c_rows = load_scale_rows("c_rows", c_scales, 64, [(0, 64), (96, 128)])
+
+        th_sb = pool.tile([P, 1], F32, name="th_sb")
+        nc.scalar.dma_start(out=th_sb[:], in_=th[0])
+
+        k_pool = pool.tile([P, T], I32, name="k_pool", align_bytes=64)
+        nc.sync.dma_start(out=k_pool[:], in_=k_words[0].rearrange("p t b -> p (t b)").bitcast(I32))
+        q_raw = pool.tile([P, PASSES, PACK, NQ], F32, name="q_raw")
+        nc.sync.dma_start(
+            out=q_raw[:].rearrange("p o j n -> p o (j n)"),
+            in_=qT[0].rearrange("(o p j) n -> p o (j n)", o=PASSES, j=PACK),
+        )
+        c_pool = pool.tile([P, T], I32, name="c_pool", align_bytes=64)
+        nc.sync.dma_start(out=c_pool[:], in_=c_words[0].rearrange("p t b -> p (t b)").bitcast(I32))
+
+        neg_th = pool.tile([P, 1], F32, name="neg_th")
+        nc.scalar.activation(out=neg_th[:], in_=th_sb[:], func=ACT.Copy, scale=-1.0)
+
+        def planes_tile(name):
+            planes = pool.tile([P, PASSES, N], U8, name=name, align_bytes=64)
+            nc.vector.memset(planes[:].rearrange("p o n -> p (o n)").bitcast(I32), 0)
+            return planes
+
+        k_planes = planes_tile("k_planes")
+        c_planes = planes_tile("c_planes")
+
+        def gather_scales(name, rows, row0, planes):
+            picked = pool.tile([P, N], U8, name=name, align_bytes=64)
+            nc.vector.tensor_copy(picked[:], rows[:].indirect(offsets[:]))
+            for quad in range(4):
+                nc.scalar.dma_start(
+                    out=planes[32 * quad : 32 * quad + 4, :, :].bitcast(I32),
+                    in_=picked[row0 + 8 * quad : row0 + 8 * quad + 8, :].bitcast(I32),
+                )
+
+        gather_scales("k_picked", k_rows, 0, k_planes)
+        gather_scales("c_picked", c_rows, 64, c_planes)
+
+        k_pairs = pool.tile([P, N], U32, name="k_pairs", align_bytes=64)
+        nc.vector.tensor_copy(k_pairs[:], k_pool[:].bitcast(U32).indirect(offsets[:]))
+
+        def part_words(words, pairs, cols):
+            nc.vector.tensor_copy(
+                out=words[:, :, cols],
+                in_=pairs[:, cols].bitcast(U16).rearrange("p (n o) -> p o n", o=PASSES),
+            )
+
+        k_split = pool.tile([P, PASSES, N], U16, name="k_split", align_bytes=64)
+        part_words(k_split, k_pairs, slice(0, N))
+
+        hi = pool.tile([P, PASSES, NQ, PACK], BF16, name="hi", align_bytes=64)
+        lo = pool.tile([P, PASSES, NQ, PACK], BF16, name="lo", align_bytes=64)
+        q_view = q_raw[:].rearrange("p o j n -> p o n j")
+        nc.scalar.activation(out=hi[:], in_=q_view, func=ACT.Relu)
+        nc.vector.tensor_scalar(out=lo[:], in0=q_view, scalar1=0.0, scalar2=None, op0=ALU.min)
+
+        def quantise(name, values):
+            codes = pool.tile([P, PASSES * NQ], U32, name=name + "_codes", align_bytes=64)
+            scales = pool.tile([P, PASSES * NQ], U8, name=name + "_scales", align_bytes=64)
+            nc.vector.quantize_mx(
+                out=codes[:].bitcast(FP8X4),
+                scales=scales[:],
+                in_=values[:].rearrange("p o n j -> p (o n j)"),
+            )
+            return codes, scales
+
+        hi_codes, hi_scales = quantise("hi", hi)
+        lo_codes, lo_scales = quantise("lo", lo)
+
+        banks = [psum.tile([P, GROUP], F32, name="bank%d" % g) for g in range(GROUPS)]
+
+        def multiply(g, codes, scales, words, planes, first):
+            cols = slice(g * GROUP, (g + 1) * GROUP)
+            for o in range(PASSES):
+                rows = slice(o * NQ, (o + 1) * NQ)
+                nc.tensor.matmul_mx(
+                    out=banks[g][:],
+                    lhsT=codes[:, rows].bitcast(FP8X4),
+                    lhsT_scale=scales[:, rows],
+                    rhs=words[:, o, cols].bitcast(FP4X4),
+                    rhs_scale=planes[:, o, cols],
+                    start=(first and o == 0),
+                    stop=(not first and o == PASSES - 1),
+                )
+
+        for g in range(GROUPS):
+            multiply(g, hi_codes, hi_scales, k_split, k_planes, True)
+
+        c_pairs = pool.tile([P, N], U32, name="c_pairs", align_bytes=64)
+        for h in range(2):
+            nc.vector.tensor_copy(
+                c_pairs[:, h * HALF : (h + 1) * HALF],
+                c_pool[:].bitcast(U32).indirect(offsets[:, h * HALF // 16 : (h + 1) * HALF // 16]),
+            )
+        c_split = pool.tile([P, PASSES, N], U16, name="c_split", align_bytes=64)
+        for g in range(GROUPS):
+            part_words(c_split, c_pairs, slice(g * GROUP, (g + 1) * GROUP))
+            multiply(g, lo_codes, lo_scales, c_split, c_planes, False)
+
+        best = pool.tile([P, N // SEG], F32, name="best")
+        runs = GROUP // SEG
+        for g in range(GROUPS):
+            nc.vector.tensor_reduce(
+                out=best[:, g * runs : (g + 1) * runs],
+                in_=banks[g][:].rearrange("p (j s) -> p j s", s=SEG),
+                axis=mybir.AxisListType.X,
+                op=ALU.max,
+            )
+        result = pool.tile([P, N // SEG], F32, name="result")
+        nc.scalar.activation(out=result[:], in_=best[:], func=ACT.Identity, bias=neg_th[:], scale=1.0)
+        nc.scalar.dma_start(out=out[0], in_=result[:])

@@ -43,8 +43,8 @@ def tile_attend_questgrp_topk_kernel(tc, qT, k_words, k_scales, c_words, c_scale
                 nc.vector.memset(rows[a:b, :].bitcast(I32), 0)
             return rows
 
-        k_rows = load_scale_rows("k_rows", k_scales, 0, [(32, 64), (64, 128)])
-        c_rows = load_scale_rows("c_rows", c_scales, 64, [(0, 64), (96, 128)])
+        k_rows = load_scale_rows("k_rows", k_scales, 96, [(0, 96)])
+        c_rows = load_scale_rows("c_rows", c_scales, 96, [(0, 96)])
 
         th_sb = pool.tile([P, 1], F32, name="th_sb")
         nc.scalar.dma_start(out=th_sb[:], in_=th[0])
@@ -64,23 +64,23 @@ def tile_attend_questgrp_topk_kernel(tc, qT, k_words, k_scales, c_words, c_scale
 
         def planes_tile(name):
             planes = pool.tile([P, PASSES, N], U8, name=name, align_bytes=64)
-            nc.vector.memset(planes[:].rearrange("p o n -> p (o n)").bitcast(I32), 0)
+            nc.gpsimd.memset(planes[:].rearrange("p o n -> p (o n)").bitcast(I32), 0)
             return planes
 
         k_planes = planes_tile("k_planes")
         c_planes = planes_tile("c_planes")
 
-        def gather_scales(name, rows, row0, planes):
+        def gather_scales(name, rows, row0, planes, queues):
             picked = pool.tile([P, N], U8, name=name, align_bytes=64)
             nc.vector.tensor_copy(picked[:], rows[:].indirect(offsets[:]))
             for quad in range(4):
-                nc.scalar.dma_start(
+                queues[quad].dma_start(
                     out=planes[32 * quad : 32 * quad + 4, :, :].bitcast(I32),
                     in_=picked[row0 + 8 * quad : row0 + 8 * quad + 8, :].bitcast(I32),
                 )
 
-        gather_scales("k_picked", k_rows, 0, k_planes)
-        gather_scales("c_picked", c_rows, 64, c_planes)
+        gather_scales("k_picked", k_rows, 96, k_planes, [nc.gpsimd, nc.scalar, nc.scalar, nc.scalar])
+        gather_scales("c_picked", c_rows, 96, c_planes, [nc.scalar] * 4)
 
         k_pairs = pool.tile([P, N], U32, name="k_pairs", align_bytes=64)
         nc.vector.tensor_copy(k_pairs[:], k_pool[:].bitcast(U32).indirect(offsets[:]))

@@ -59,28 +59,27 @@ def tile_attend_questgrp_topk_kernel(tc, qT, k_words, k_scales, c_words, c_scale
         c_pool = pool.tile([P, T], I32, name="c_pool", align_bytes=64)
         nc.sync.dma_start(out=c_pool[:], in_=c_words[0].rearrange("p t b -> p (t b)").bitcast(I32))
 
+        planes = pool.tile([P, PASSES, 2, N], U8, name="planes", align_bytes=64)
+        nc.gpsimd.memset(planes[:].rearrange("p o s n -> p (o s n)").bitcast(I32), 0)
+
         neg_th = pool.tile([P, 1], F32, name="neg_th")
         nc.scalar.activation(out=neg_th[:], in_=th_sb[:], func=ACT.Copy, scale=-1.0)
 
-        def planes_tile(name):
-            planes = pool.tile([P, PASSES, N], U8, name=name, align_bytes=64)
-            nc.gpsimd.memset(planes[:].rearrange("p o n -> p (o n)").bitcast(I32), 0)
-            return planes
+        picked = pool.tile([P, 2, N], U8, name="picked", align_bytes=64)
+        nc.vector.tensor_copy(picked[:, 0, :], k_rows[:].indirect(offsets[:]))
+        nc.vector.tensor_copy(picked[:, 1, :], c_rows[:].indirect(offsets[:]))
 
-        k_planes = planes_tile("k_planes")
-        c_planes = planes_tile("c_planes")
+        def spread(quad, sides):
+            nc.sync.dma_start(
+                out=planes[32 * quad : 32 * quad + 4, :, sides, :].rearrange("p o s n -> p o (s n)").bitcast(I32),
+                in_=picked[96 + 8 * quad : 96 + 8 * quad + 8, sides, :].rearrange("p s n -> p (s n)").bitcast(I32),
+            )
 
-        def gather_scales(name, rows, row0, planes, queues):
-            picked = pool.tile([P, N], U8, name=name, align_bytes=64)
-            nc.vector.tensor_copy(picked[:], rows[:].indirect(offsets[:]))
-            for quad in range(4):
-                queues[quad].dma_start(
-                    out=planes[32 * quad : 32 * quad + 4, :, :].bitcast(I32),
-                    in_=picked[row0 + 8 * quad : row0 + 8 * quad + 8, :].bitcast(I32),
-                )
-
-        gather_scales("k_picked", k_rows, 96, k_planes, [nc.gpsimd, nc.scalar, nc.scalar, nc.scalar])
-        gather_scales("c_picked", c_rows, 96, c_planes, [nc.scalar] * 4)
+        for quad in range(3):
+            spread(quad, slice(0, 1))
+        spread(3, slice(0, 2))
+        for quad in range(3):
+            spread(quad, slice(1, 2))
 
         k_pairs = pool.tile([P, N], U32, name="k_pairs", align_bytes=64)
         nc.vector.tensor_copy(k_pairs[:], k_pool[:].bitcast(U32).indirect(offsets[:]))
@@ -115,7 +114,7 @@ def tile_attend_questgrp_topk_kernel(tc, qT, k_words, k_scales, c_words, c_scale
 
         banks = [psum.tile([P, GROUP], F32, name="bank%d" % g) for g in range(GROUPS)]
 
-        def multiply(g, codes, scales, words, planes, first):
+        def multiply(g, codes, scales, words, side, first):
             cols = slice(g * GROUP, (g + 1) * GROUP)
             for o in range(PASSES):
                 rows = slice(o * NQ, (o + 1) * NQ)
@@ -124,13 +123,13 @@ def tile_attend_questgrp_topk_kernel(tc, qT, k_words, k_scales, c_words, c_scale
                     lhsT=codes[:, rows].bitcast(FP8X4),
                     lhsT_scale=scales[:, rows],
                     rhs=words[:, o, cols].bitcast(FP4X4),
-                    rhs_scale=planes[:, o, cols],
+                    rhs_scale=planes[:, o, side, cols],
                     start=(first and o == 0),
                     stop=(not first and o == PASSES - 1),
                 )
 
         for g in range(GROUPS):
-            multiply(g, hi_codes, hi_scales, k_split, k_planes, True)
+            multiply(g, hi_codes, hi_scales, k_split, 0, True)
 
         c_pairs = pool.tile([P, N], U32, name="c_pairs", align_bytes=64)
         for h in range(2):
@@ -141,7 +140,7 @@ def tile_attend_questgrp_topk_kernel(tc, qT, k_words, k_scales, c_words, c_scale
         c_split = pool.tile([P, PASSES, N], U16, name="c_split", align_bytes=64)
         for g in range(GROUPS):
             part_words(c_split, c_pairs, slice(g * GROUP, (g + 1) * GROUP))
-            multiply(g, lo_codes, lo_scales, c_split, c_planes, False)
+            multiply(g, lo_codes, lo_scales, c_split, 1, False)
 
         best = pool.tile([P, N // SEG], F32, name="best")
         runs = GROUP // SEG

@@ -46,12 +46,9 @@ def tile_attend_questgrp_topk_kernel(tc, qT, k_words, k_scales, c_words, c_scale
         k_rows = load_scale_rows("k_rows", k_scales, 96, [(0, 96)])
         c_rows = load_scale_rows("c_rows", c_scales, 96, [(0, 96)])
 
-        th_sb = pool.tile([P, 1], F32, name="th_sb")
-        nc.scalar.dma_start(out=th_sb[:], in_=th[0])
-
         k_pool = pool.tile([P, T], I32, name="k_pool", align_bytes=64)
         nc.sync.dma_start(out=k_pool[:], in_=k_words[0].rearrange("p t b -> p (t b)").bitcast(I32))
-        q_raw = pool.tile([P, PASSES, PACK, NQ], F32, name="q_raw")
+        q_raw = pool.tile([P, PASSES, PACK, NQ], F32, name="q_raw", tag="q_then_th")
         nc.sync.dma_start(
             out=q_raw[:].rearrange("p o j n -> p o (j n)"),
             in_=qT[0].rearrange("(o p j) n -> p o (j n)", o=PASSES, j=PACK),
@@ -62,8 +59,10 @@ def tile_attend_questgrp_topk_kernel(tc, qT, k_words, k_scales, c_words, c_scale
         planes = pool.tile([P, PASSES, 2, N], U8, name="planes", align_bytes=64)
         nc.gpsimd.memset(planes[:].rearrange("p o s n -> p (o s n)").bitcast(I32), 0)
 
-        neg_th = pool.tile([P, 1], F32, name="neg_th")
-        nc.scalar.activation(out=neg_th[:], in_=th_sb[:], func=ACT.Copy, scale=-1.0)
+        blank = pool.tile([P, 1], F32, name="blank")
+        nc.gpsimd.memset(blank[:], 0.0)
+        zero = pool.tile([P, 1], F32, name="zero")
+        nc.scalar.activation(out=zero[:], in_=blank[:], func=ACT.Relu)
 
         picked = pool.tile([P, 2, N], U8, name="picked", align_bytes=64)
         nc.vector.tensor_copy(picked[:, 0, :], k_rows[:].indirect(offsets[:]))
@@ -75,10 +74,11 @@ def tile_attend_questgrp_topk_kernel(tc, qT, k_words, k_scales, c_words, c_scale
                 in_=picked[96 + 8 * quad : 96 + 8 * quad + 8, sides, :].rearrange("p s n -> p (s n)").bitcast(I32),
             )
 
-        for quad in range(3):
+        for quad in (0, 2):
             spread(quad, slice(0, 1))
-        spread(3, slice(0, 2))
-        for quad in range(3):
+        for quad in (1, 3):
+            spread(quad, slice(0, 2))
+        for quad in (0, 2):
             spread(quad, slice(1, 2))
 
         k_pairs = pool.tile([P, N], U32, name="k_pairs", align_bytes=64)
@@ -91,13 +91,18 @@ def tile_attend_questgrp_topk_kernel(tc, qT, k_words, k_scales, c_words, c_scale
             )
 
         k_split = pool.tile([P, PASSES, N], U16, name="k_split", align_bytes=64)
-        part_words(k_split, k_pairs, slice(0, N))
 
         hi = pool.tile([P, PASSES, NQ, PACK], BF16, name="hi", align_bytes=64)
         lo = pool.tile([P, PASSES, NQ, PACK], BF16, name="lo", align_bytes=64)
         q_view = q_raw[:].rearrange("p o j n -> p o n j")
-        nc.scalar.activation(out=hi[:], in_=q_view, func=ACT.Relu)
+        nc.scalar.activation(out=hi[:], in_=q_view, func=ACT.Relu, bias=zero[:], scale=1.0)
         nc.vector.tensor_scalar(out=lo[:], in0=q_view, scalar1=0.0, scalar2=None, op0=ALU.min)
+        part_words(k_split, k_pairs, slice(0, N))
+
+        th_sb = pool.tile([P, 1], F32, name="th_sb", tag="q_then_th")
+        nc.sync.dma_start(out=th_sb[:], in_=th[0])
+        neg_th = pool.tile([P, 1], F32, name="neg_th")
+        nc.scalar.activation(out=neg_th[:], in_=th_sb[:], func=ACT.Copy, scale=-1.0)
 
         def quantise(name, values):
             codes = pool.tile([P, PASSES * NQ], U32, name=name + "_codes", align_bytes=64)

@@ -46,13 +46,13 @@ def tile_attend_questgrp_topk_kernel(tc, qT, k_words, k_scales, c_words, c_scale
         k_rows = load_scale_rows("k_rows", k_scales, 96, [(0, 96)])
         c_rows = load_scale_rows("c_rows", c_scales, 96, [(0, 96)])
 
-        k_pool = pool.tile([P, T], I32, name="k_pool", align_bytes=64)
-        nc.sync.dma_start(out=k_pool[:], in_=k_words[0].rearrange("p t b -> p (t b)").bitcast(I32))
         q_raw = pool.tile([P, PASSES, PACK, NQ], F32, name="q_raw", tag="q_then_th")
         nc.sync.dma_start(
             out=q_raw[:].rearrange("p o j n -> p o (j n)"),
             in_=qT[0].rearrange("(o p j) n -> p o (j n)", o=PASSES, j=PACK),
         )
+        k_pool = pool.tile([P, T], I32, name="k_pool", align_bytes=64)
+        nc.sync.dma_start(out=k_pool[:], in_=k_words[0].rearrange("p t b -> p (t b)").bitcast(I32))
         c_pool = pool.tile([P, T], I32, name="c_pool", align_bytes=64)
         nc.sync.dma_start(out=c_pool[:], in_=c_words[0].rearrange("p t b -> p (t b)").bitcast(I32))
 
@@ -81,8 +81,6 @@ def tile_attend_questgrp_topk_kernel(tc, qT, k_words, k_scales, c_words, c_scale
         for quad in (0, 2):
             spread(quad, slice(1, 2))
 
-        k_pairs = pool.tile([P, N], U32, name="k_pairs", align_bytes=64)
-        nc.vector.tensor_copy(k_pairs[:], k_pool[:].bitcast(U32).indirect(offsets[:]))
 
         def part_words(words, pairs, cols):
             nc.vector.tensor_copy(
@@ -96,8 +94,9 @@ def tile_attend_questgrp_topk_kernel(tc, qT, k_words, k_scales, c_words, c_scale
         lo = pool.tile([P, PASSES, NQ, PACK], BF16, name="lo", align_bytes=64)
         q_view = q_raw[:].rearrange("p o j n -> p o n j")
         nc.scalar.activation(out=hi[:], in_=q_view, func=ACT.Relu, bias=zero[:], scale=1.0)
-        nc.vector.tensor_scalar(out=lo[:], in0=q_view, scalar1=0.0, scalar2=None, op0=ALU.min)
-        part_words(k_split, k_pairs, slice(0, N))
+        neg_lo = pool.tile([P, PASSES, NQ, PACK], BF16, name="neg_lo", align_bytes=64)
+        nc.scalar.activation(out=neg_lo[:], in_=q_view, func=ACT.Relu, bias=zero[:], scale=-1.0)
+        nc.scalar.activation(out=lo[:], in_=neg_lo[:], func=ACT.Copy, scale=-1.0)
 
         th_sb = pool.tile([P, 1], F32, name="th_sb", tag="q_then_th")
         nc.sync.dma_start(out=th_sb[:], in_=th[0])
@@ -115,6 +114,9 @@ def tile_attend_questgrp_topk_kernel(tc, qT, k_words, k_scales, c_words, c_scale
             return codes, scales
 
         hi_codes, hi_scales = quantise("hi", hi)
+        k_pairs = pool.tile([P, N], U32, name="k_pairs", align_bytes=64)
+        nc.vector.tensor_copy(k_pairs[:], k_pool[:].bitcast(U32).indirect(offsets[:]))
+        part_words(k_split, k_pairs, slice(0, N))
         lo_codes, lo_scales = quantise("lo", lo)
 
         banks = [psum.tile([P, GROUP], F32, name="bank%d" % g) for g in range(GROUPS)]

@@ -22,6 +22,7 @@ PASSES = D // (P * PACK)
 GROUP = 128
 GROUPS = N // GROUP
 HALF = N // 2
+K_SIDE, C_SIDE = 0, 1
 
 
 def tile_attend_questgrp_topk_kernel(tc, qT, k_words, k_scales, c_words, c_scales, th, offs, out):
@@ -43,21 +44,30 @@ def tile_attend_questgrp_topk_kernel(tc, qT, k_words, k_scales, c_words, c_scale
                 nc.vector.memset(rows[a:b, :].bitcast(I32), 0)
             return rows
 
-        k_rows = load_scale_rows("k_rows", k_scales, 96, [(0, 96)])
-        c_rows = load_scale_rows("c_rows", c_scales, 96, [(0, 96)])
+        k_row0, c_row0 = 96, 32
+        k_rows = load_scale_rows("k_rows", k_scales, k_row0, [(0, 96)])
+        c_rows = load_scale_rows("c_rows", c_scales, c_row0, [(0, 32), (64, 128)])
 
-        q_raw = pool.tile([P, PASSES, PACK, NQ], F32, name="q_raw", tag="q_then_th")
-        nc.sync.dma_start(
-            out=q_raw[:].rearrange("p o j n -> p o (j n)"),
-            in_=qT[0].rearrange("(o p j) n -> p o (j n)", o=PASSES, j=PACK),
-        )
-        k_pool = pool.tile([P, T], I32, name="k_pool", align_bytes=64)
-        nc.sync.dma_start(out=k_pool[:], in_=k_words[0].rearrange("p t b -> p (t b)").bitcast(I32))
-        c_pool = pool.tile([P, T], I32, name="c_pool", align_bytes=64)
-        nc.sync.dma_start(out=c_pool[:], in_=c_words[0].rearrange("p t b -> p (t b)").bitcast(I32))
+        def load_q(o, tag):
+            raw = pool.tile([P, PACK, NQ], F32, name="q_raw%d" % o, tag=tag)
+            nc.sync.dma_start(
+                out=raw[:].rearrange("p j n -> p (j n)"),
+                in_=qT[0, o * P * PACK : (o + 1) * P * PACK, :].rearrange("(p j) n -> p (j n)", j=PACK),
+            )
+            return raw
 
-        planes = pool.tile([P, PASSES, 2, N], U8, name="planes", align_bytes=64)
-        nc.gpsimd.memset(planes[:].rearrange("p o s n -> p (o s n)").bitcast(I32), 0)
+        def load_words(name, words, tag):
+            held = pool.tile([P, T], I32, name=name, tag=tag, align_bytes=64)
+            nc.sync.dma_start(out=held[:], in_=words[0].rearrange("p t b -> p (t b)").bitcast(I32))
+            return held
+
+        q_raw = [load_q(0, "q_raw0")]
+        k_pool = load_words("k_pool", k_words, "k_pool")
+        q_raw.append(load_q(1, "q_then_th"))
+        c_pool = load_words("c_pool", c_words, "c_pool")
+
+        planes = pool.tile([P, 2, PASSES, N], U8, name="planes", align_bytes=64)
+        nc.gpsimd.memset(planes[:].rearrange("p s o n -> p (s o n)").bitcast(I32), 0)
 
         blank = pool.tile([P, 1], F32, name="blank")
         nc.gpsimd.memset(blank[:], 0.0)
@@ -65,22 +75,36 @@ def tile_attend_questgrp_topk_kernel(tc, qT, k_words, k_scales, c_words, c_scale
         nc.scalar.activation(out=zero[:], in_=blank[:], func=ACT.Relu)
 
         picked = pool.tile([P, 2, N], U8, name="picked", align_bytes=64)
-        nc.vector.tensor_copy(picked[:, 0, :], k_rows[:].indirect(offsets[:]))
-        nc.vector.tensor_copy(picked[:, 1, :], c_rows[:].indirect(offsets[:]))
+        nc.vector.tensor_copy(picked[:, K_SIDE, :], k_rows[:].indirect(offsets[:]))
+        nc.vector.tensor_copy(picked[:, C_SIDE, :], c_rows[:].indirect(offsets[:]))
 
-        def spread(quad, sides):
-            nc.sync.dma_start(
-                out=planes[32 * quad : 32 * quad + 4, :, sides, :].rearrange("p o s n -> p o (s n)").bitcast(I32),
-                in_=picked[96 + 8 * quad : 96 + 8 * quad + 8, sides, :].rearrange("p s n -> p (s n)").bitcast(I32),
+        def spread(queues, side, row0):
+            for quad, queue in zip(range(4), queues):
+                queue.dma_start(
+                    out=planes[32 * quad : 32 * quad + 4, side].bitcast(I32),
+                    in_=picked[row0 + 8 * quad : row0 + 8 * quad + 8, side, :].bitcast(I32),
+                )
+
+        spread([nc.sync] * 4, K_SIDE, k_row0)
+        spread([nc.sync, nc.sync, nc.sync, nc.gpsimd], C_SIDE, c_row0)
+
+        parts = pool.tile([P, PASSES, 2, NQ, PACK], BF16, name="parts", align_bytes=64)
+        codes = pool.tile([P, PASSES, 2, NQ], U32, name="codes", align_bytes=64)
+        scales = pool.tile([P, PASSES, 2, NQ], U8, name="scales", align_bytes=64)
+
+        def part_q(o):
+            view = q_raw[o][:].rearrange("p j n -> p n j")
+            flipped = pool.tile([P, NQ, PACK], BF16, name="flipped%d" % o, align_bytes=64)
+            nc.scalar.activation(out=flipped[:], in_=view, func=ACT.Relu, bias=zero[:], scale=-1.0)
+            nc.scalar.activation(out=parts[:, o, K_SIDE], in_=view, func=ACT.Relu, bias=zero[:], scale=1.0)
+            return flipped
+
+        def quantise(o):
+            nc.vector.quantize_mx(
+                out=codes[:, o].rearrange("p s n -> p (s n)").bitcast(FP8X4),
+                scales=scales[:, o].rearrange("p s n -> p (s n)"),
+                in_=parts[:, o].rearrange("p s n j -> p (s n j)"),
             )
-
-        for quad in (0, 2):
-            spread(quad, slice(0, 1))
-        for quad in (1, 3):
-            spread(quad, slice(0, 2))
-        for quad in (0, 2):
-            spread(quad, slice(1, 2))
-
 
         def part_words(words, pairs, cols):
             nc.vector.tensor_copy(
@@ -88,55 +112,40 @@ def tile_attend_questgrp_topk_kernel(tc, qT, k_words, k_scales, c_words, c_scale
                 in_=pairs[:, cols].bitcast(U16).rearrange("p (n o) -> p o n", o=PASSES),
             )
 
-        k_split = pool.tile([P, PASSES, N], U16, name="k_split", align_bytes=64)
+        flipped = part_q(0)
+        nc.scalar.activation(out=parts[:, 0, C_SIDE], in_=flipped[:], func=ACT.Copy, scale=-1.0)
+        quantise(0)
 
-        hi = pool.tile([P, PASSES, NQ, PACK], BF16, name="hi", align_bytes=64)
-        lo = pool.tile([P, PASSES, NQ, PACK], BF16, name="lo", align_bytes=64)
-        q_view = q_raw[:].rearrange("p o j n -> p o n j")
-        nc.scalar.activation(out=hi[:], in_=q_view, func=ACT.Relu, bias=zero[:], scale=1.0)
-        neg_lo = pool.tile([P, PASSES, NQ, PACK], BF16, name="neg_lo", align_bytes=64)
-        nc.scalar.activation(out=neg_lo[:], in_=q_view, func=ACT.Relu, bias=zero[:], scale=-1.0)
-        nc.scalar.activation(out=lo[:], in_=neg_lo[:], func=ACT.Copy, scale=-1.0)
+        k_pairs = pool.tile([P, N], U32, name="k_pairs", align_bytes=64)
+        nc.vector.tensor_copy(k_pairs[:], k_pool[:].bitcast(U32).indirect(offsets[:]))
+        flipped = part_q(1)
+        nc.vector.tensor_scalar(out=parts[:, 1, C_SIDE], in0=flipped[:], scalar1=-1.0, scalar2=None, op0=ALU.mult)
+        k_split = pool.tile([P, PASSES, N], U16, name="k_split", tag="flipped1", align_bytes=64)
+        part_words(k_split, k_pairs, slice(0, N))
+        quantise(1)
 
         th_sb = pool.tile([P, 1], F32, name="th_sb", tag="q_then_th")
         nc.sync.dma_start(out=th_sb[:], in_=th[0])
         neg_th = pool.tile([P, 1], F32, name="neg_th")
         nc.scalar.activation(out=neg_th[:], in_=th_sb[:], func=ACT.Copy, scale=-1.0)
 
-        def quantise(name, values):
-            codes = pool.tile([P, PASSES * NQ], U32, name=name + "_codes", align_bytes=64)
-            scales = pool.tile([P, PASSES * NQ], U8, name=name + "_scales", align_bytes=64)
-            nc.vector.quantize_mx(
-                out=codes[:].bitcast(FP8X4),
-                scales=scales[:],
-                in_=values[:].rearrange("p o n j -> p (o n j)"),
-            )
-            return codes, scales
-
-        hi_codes, hi_scales = quantise("hi", hi)
-        k_pairs = pool.tile([P, N], U32, name="k_pairs", align_bytes=64)
-        nc.vector.tensor_copy(k_pairs[:], k_pool[:].bitcast(U32).indirect(offsets[:]))
-        part_words(k_split, k_pairs, slice(0, N))
-        lo_codes, lo_scales = quantise("lo", lo)
-
         banks = [psum.tile([P, GROUP], F32, name="bank%d" % g) for g in range(GROUPS)]
 
-        def multiply(g, codes, scales, words, side, first):
+        def multiply(g, o, words, side):
             cols = slice(g * GROUP, (g + 1) * GROUP)
-            for o in range(PASSES):
-                rows = slice(o * NQ, (o + 1) * NQ)
-                nc.tensor.matmul_mx(
-                    out=banks[g][:],
-                    lhsT=codes[:, rows].bitcast(FP8X4),
-                    lhsT_scale=scales[:, rows],
-                    rhs=words[:, o, cols].bitcast(FP4X4),
-                    rhs_scale=planes[:, o, side, cols],
-                    start=(first and o == 0),
-                    stop=(not first and o == PASSES - 1),
-                )
+            nc.tensor.matmul_mx(
+                out=banks[g][:],
+                lhsT=codes[:, o, side].bitcast(FP8X4),
+                lhsT_scale=scales[:, o, side],
+                rhs=words[:, o, cols].bitcast(FP4X4),
+                rhs_scale=planes[:, side, o, cols],
+                start=(side == K_SIDE and o == 0),
+                stop=(side == C_SIDE and o == PASSES - 1),
+            )
 
-        for g in range(GROUPS):
-            multiply(g, hi_codes, hi_scales, k_split, 0, True)
+        for o in range(PASSES):
+            for g in range(GROUPS):
+                multiply(g, o, k_split, K_SIDE)
 
         c_pairs = pool.tile([P, N], U32, name="c_pairs", align_bytes=64)
         for h in range(2):
@@ -147,7 +156,8 @@ def tile_attend_questgrp_topk_kernel(tc, qT, k_words, k_scales, c_words, c_scale
         c_split = pool.tile([P, PASSES, N], U16, name="c_split", align_bytes=64)
         for g in range(GROUPS):
             part_words(c_split, c_pairs, slice(g * GROUP, (g + 1) * GROUP))
-            multiply(g, lo_codes, lo_scales, c_split, 1, False)
+            for o in range(PASSES):
+                multiply(g, o, c_split, C_SIDE)
 
         best = pool.tile([P, N // SEG], F32, name="best")
         runs = GROUP // SEG

@@ -79,14 +79,14 @@ def tile_attend_questgrp_topk_kernel(tc, qT, k_words, k_scales, c_words, c_scale
         nc.vector.tensor_copy(picked[:, C_SIDE, :], c_rows[:].indirect(offsets[:]))
 
         def spread(queues, side, row0):
-            for quad, queue in zip(range(4), queues):
+            for quad, queue in zip((0, 2, 1, 3), queues):
                 queue.dma_start(
                     out=planes[32 * quad : 32 * quad + 4, side].bitcast(I32),
                     in_=picked[row0 + 8 * quad : row0 + 8 * quad + 8, side, :].bitcast(I32),
                 )
 
         spread([nc.sync] * 4, K_SIDE, k_row0)
-        spread([nc.sync, nc.sync, nc.sync, nc.gpsimd], C_SIDE, c_row0)
+        spread([nc.sync] * 4, C_SIDE, c_row0)
 
         parts = pool.tile([P, PASSES, 2, NQ, PACK], BF16, name="parts", align_bytes=64)
         codes = pool.tile([P, PASSES, 2, NQ], U32, name="codes", align_bytes=64)
@@ -126,8 +126,6 @@ def tile_attend_questgrp_topk_kernel(tc, qT, k_words, k_scales, c_words, c_scale
 
         th_sb = pool.tile([P, 1], F32, name="th_sb", tag="q_then_th")
         nc.sync.dma_start(out=th_sb[:], in_=th[0])
-        neg_th = pool.tile([P, 1], F32, name="neg_th")
-        nc.scalar.activation(out=neg_th[:], in_=th_sb[:], func=ACT.Copy, scale=-1.0)
 
         banks = [psum.tile([P, GROUP], F32, name="bank%d" % g) for g in range(GROUPS)]
 
@@ -169,5 +167,5 @@ def tile_attend_questgrp_topk_kernel(tc, qT, k_words, k_scales, c_words, c_scale
                 op=ALU.max,
             )
         result = pool.tile([P, N // SEG], F32, name="result")
-        nc.scalar.activation(out=result[:], in_=best[:], func=ACT.Identity, bias=neg_th[:], scale=1.0)
-        nc.scalar.dma_start(out=out[0], in_=result[:])
+        nc.vector.tensor_scalar(out=result[:], in0=best[:], scalar1=th_sb[:], scalar2=None, op0=ALU.subtract)
+        nc.sync.dma_start(out=out[0], in_=result[:])

@@ -34,19 +34,19 @@ def tile_attend_questgrp_topk_kernel(tc, qT, k_words, k_scales, c_words, c_scale
         offsets = pool.tile([P, N // 16], U16, name="offsets")
         nc.sync.dma_start(offsets[:], offs)
 
-        def load_scale_rows(name, scales, row0, empty):
+        def load_scale_rows(name, scales, row0, empty, clearer):
             rows = pool.tile([P, T], U8, name=name, align_bytes=64)
             nc.sync.dma_start(
                 out=rows[row0 : row0 + 32, :].bitcast(I32),
                 in_=scales.bitcast(I32).rearrange("o f t -> f o t"),
             )
             for a, b in empty:
-                nc.vector.memset(rows[a:b, :].bitcast(I32), 0)
+                clearer.memset(rows[a:b, :].bitcast(I32), 0)
             return rows
 
         k_row0, c_row0 = 96, 32
-        k_rows = load_scale_rows("k_rows", k_scales, k_row0, [(0, 96)])
-        c_rows = load_scale_rows("c_rows", c_scales, c_row0, [(0, 32), (64, 128)])
+        k_rows = load_scale_rows("k_rows", k_scales, k_row0, [(0, 96)], nc.vector)
+        c_rows = load_scale_rows("c_rows", c_scales, c_row0, [(0, 32), (64, 128)], nc.gpsimd)
 
         def load_q(o, tag):
             raw = pool.tile([P, PACK, NQ], F32, name="q_raw%d" % o, tag=tag)
@@ -86,7 +86,7 @@ def tile_attend_questgrp_topk_kernel(tc, qT, k_words, k_scales, c_words, c_scale
                 )
 
         spread([nc.sync] * 4, K_SIDE, k_row0)
-        spread([nc.sync] * 4, C_SIDE, c_row0)
+        spread([nc.sync, nc.sync, nc.sync, nc.gpsimd], C_SIDE, c_row0)
 
         parts = pool.tile([P, PASSES, 2, NQ, PACK], BF16, name="parts", align_bytes=64)
         codes = pool.tile([P, PASSES, 2, NQ], U32, name="codes", align_bytes=64)

@@ -44,9 +44,9 @@ def tile_attend_questgrp_topk_kernel(tc, qT, k_words, k_scales, c_words, c_scale
                 clearer.memset(rows[a:b, :].bitcast(I32), 0)
             return rows
 
-        k_row0, c_row0 = 96, 32
-        k_rows = load_scale_rows("k_rows", k_scales, k_row0, [(0, 96)], nc.vector)
-        c_rows = load_scale_rows("c_rows", c_scales, c_row0, [(0, 32), (64, 128)], nc.gpsimd)
+        row0 = 96
+        k_rows = load_scale_rows("k_rows", k_scales, row0, [(0, 96)], nc.vector)
+        c_rows = load_scale_rows("c_rows", c_scales, row0, [(0, 96)], nc.gpsimd)
 
         def load_q(o, tag):
             raw = pool.tile([P, PACK, NQ], F32, name="q_raw%d" % o, tag=tag)
@@ -66,8 +66,8 @@ def tile_attend_questgrp_topk_kernel(tc, qT, k_words, k_scales, c_words, c_scale
         q_raw.append(load_q(1, "q_then_th"))
         c_pool = load_words("c_pool", c_words, "c_pool")
 
-        planes = pool.tile([P, 2, PASSES, N], U8, name="planes", align_bytes=64)
-        nc.gpsimd.memset(planes[:].rearrange("p s o n -> p (s o n)").bitcast(I32), 0)
+        planes = pool.tile([P, PASSES, 2, N], U8, name="planes", align_bytes=64)
+        nc.gpsimd.memset(planes[:].rearrange("p o s n -> p (o s n)").bitcast(I32), 0)
 
         blank = pool.tile([P, 1], F32, name="blank")
         nc.gpsimd.memset(blank[:], 0.0)
@@ -78,15 +78,17 @@ def tile_attend_questgrp_topk_kernel(tc, qT, k_words, k_scales, c_words, c_scale
         nc.vector.tensor_copy(picked[:, K_SIDE, :], k_rows[:].indirect(offsets[:]))
         nc.vector.tensor_copy(picked[:, C_SIDE, :], c_rows[:].indirect(offsets[:]))
 
-        def spread(queues, side, row0):
-            for quad, queue in zip((0, 2, 1, 3), queues):
-                queue.dma_start(
-                    out=planes[32 * quad : 32 * quad + 4, side].bitcast(I32),
-                    in_=picked[row0 + 8 * quad : row0 + 8 * quad + 8, side, :].bitcast(I32),
-                )
+        def spread(quad, sides):
+            nc.sync.dma_start(
+                out=planes[32 * quad : 32 * quad + 4, :, sides, :].rearrange("p o s n -> p o (s n)").bitcast(I32),
+                in_=picked[row0 + 8 * quad : row0 + 8 * quad + 8, sides, :].rearrange("p s n -> p (s n)").bitcast(I32),
+            )
 
-        spread([nc.sync] * 4, K_SIDE, k_row0)
-        spread([nc.sync, nc.sync, nc.sync, nc.gpsimd], C_SIDE, c_row0)
+        for quad in (0, 2, 1):
+            spread(quad, slice(K_SIDE, K_SIDE + 1))
+        spread(3, slice(0, 2))
+        for quad in (0, 1, 2):
+            spread(quad, slice(C_SIDE, C_SIDE + 1))
 
         parts = pool.tile([P, PASSES, 2, NQ, PACK], BF16, name="parts", align_bytes=64)
         codes = pool.tile([P, PASSES, 2, NQ], U32, name="codes", align_bytes=64)
@@ -136,7 +138,7 @@ def tile_attend_questgrp_topk_kernel(tc, qT, k_words, k_scales, c_words, c_scale
                 lhsT=codes[:, o, side].bitcast(FP8X4),
                 lhsT_scale=scales[:, o, side],
                 rhs=words[:, o, cols].bitcast(FP4X4),
-                rhs_scale=planes[:, side, o, cols],
+                rhs_scale=planes[:, o, side, cols],
                 start=(side == K_SIDE and o == 0),
                 stop=(side == C_SIDE and o == PASSES - 1),
             )

@@ -35,7 +35,7 @@ def tile_attend_questgrp_topk_kernel(tc, qT, k_words, k_scales, c_words, c_scale
         nc.sync.dma_start(offsets[:], offs)
 
         def load_scale_rows(name, scales, row0, empty, clearer):
-            rows = pool.tile([P, T], U8, name=name, align_bytes=64)
+            rows = pool.tile([P, T], U8, name=name, tag=name, align_bytes=64)
             nc.sync.dma_start(
                 out=rows[row0 : row0 + 32, :].bitcast(I32),
                 in_=scales.bitcast(I32).rearrange("o f t -> f o t"),
@@ -66,9 +66,6 @@ def tile_attend_questgrp_topk_kernel(tc, qT, k_words, k_scales, c_words, c_scale
         q_raw.append(load_q(1, "q_then_th"))
         c_pool = load_words("c_pool", c_words, "c_pool")
 
-        planes = pool.tile([P, PASSES, 2, N], U8, name="planes", align_bytes=64)
-        nc.gpsimd.memset(planes[:].rearrange("p o s n -> p (o s n)").bitcast(I32), 0)
-
         blank = pool.tile([P, 1], F32, name="blank")
         nc.gpsimd.memset(blank[:], 0.0)
         zero = pool.tile([P, 1], F32, name="zero")
@@ -77,6 +74,8 @@ def tile_attend_questgrp_topk_kernel(tc, qT, k_words, k_scales, c_words, c_scale
         picked = pool.tile([P, 2, N], U8, name="picked", align_bytes=64)
         nc.vector.tensor_copy(picked[:, K_SIDE, :], k_rows[:].indirect(offsets[:]))
         nc.vector.tensor_copy(picked[:, C_SIDE, :], c_rows[:].indirect(offsets[:]))
+
+        planes = pool.tile([P, PASSES, 2, N], U8, name="planes", tag="k_rows", align_bytes=64)
 
         def spread(quad, sides):
             nc.sync.dma_start(
@@ -120,6 +119,16 @@ def tile_attend_questgrp_topk_kernel(tc, qT, k_words, k_scales, c_words, c_scale
 
         k_pairs = pool.tile([P, N], U32, name="k_pairs", align_bytes=64)
         nc.vector.tensor_copy(k_pairs[:], k_pool[:].bitcast(U32).indirect(offsets[:]))
+        spare = psum.tile([P, N], F32, name="spare")
+        nc.tensor.matmul_mx(
+            out=spare[:],
+            lhsT=codes[:, 0, K_SIDE].bitcast(FP8X4),
+            lhsT_scale=scales[:, 0, K_SIDE],
+            rhs=k_pairs[:, 0:HALF].bitcast(U16).bitcast(FP4X4),
+            rhs_scale=picked[:, K_SIDE, :],
+            start=True,
+            stop=True,
+        )
         flipped = part_q(1)
         nc.vector.tensor_scalar(out=parts[:, 1, C_SIDE], in0=flipped[:], scalar1=-1.0, scalar2=None, op0=ALU.mult)
         k_split = pool.tile([P, PASSES, N], U16, name="k_split", tag="flipped1", align_bytes=64)

@@ -68,7 +68,7 @@ def tile_attend_questgrp_topk_kernel(tc, qT, k_words, k_scales, c_words, c_scale
 
         blank = pool.tile([P, 1], F32, name="blank")
         nc.gpsimd.memset(blank[:], 0.0)
-        zero = pool.tile([P, 1], F32, name="zero")
+        zero = pool.tile([P, 1], F32, name="zero", tag="zero", align_bytes=64)
         nc.scalar.activation(out=zero[:], in_=blank[:], func=ACT.Relu)
 
         picked = pool.tile([P, 2, N], U8, name="picked", align_bytes=64)
@@ -93,11 +93,11 @@ def tile_attend_questgrp_topk_kernel(tc, qT, k_words, k_scales, c_words, c_scale
         codes = pool.tile([P, PASSES, 2, NQ], U32, name="codes", align_bytes=64)
         scales = pool.tile([P, PASSES, 2, NQ], U8, name="scales", align_bytes=64)
 
-        def part_q(o):
+        def part_q(o, last_bias):
             view = q_raw[o][:].rearrange("p j n -> p n j")
             flipped = pool.tile([P, NQ, PACK], BF16, name="flipped%d" % o, align_bytes=64)
             nc.scalar.activation(out=flipped[:], in_=view, func=ACT.Relu, bias=zero[:], scale=-1.0)
-            nc.scalar.activation(out=parts[:, o, K_SIDE], in_=view, func=ACT.Relu, bias=zero[:], scale=1.0)
+            nc.scalar.activation(out=parts[:, o, K_SIDE], in_=view, func=ACT.Relu, bias=last_bias[:], scale=1.0)
             return flipped
 
         def quantise(o):
@@ -113,7 +113,7 @@ def tile_attend_questgrp_topk_kernel(tc, qT, k_words, k_scales, c_words, c_scale
                 in_=pairs[:, cols].bitcast(U16).rearrange("p (n o) -> p o n", o=PASSES),
             )
 
-        flipped = part_q(0)
+        flipped = part_q(0, zero)
         nc.scalar.activation(out=parts[:, 0, C_SIDE], in_=flipped[:], func=ACT.Copy, scale=-1.0)
         quantise(0)
 
@@ -129,9 +129,9 @@ def tile_attend_questgrp_topk_kernel(tc, qT, k_words, k_scales, c_words, c_scale
             start=True,
             stop=True,
         )
-        flipped = part_q(1)
+        flipped = part_q(1, blank)
         nc.vector.tensor_scalar(out=parts[:, 1, C_SIDE], in0=flipped[:], scalar1=-1.0, scalar2=None, op0=ALU.mult)
-        k_split = pool.tile([P, PASSES, N], U16, name="k_split", tag="flipped1", align_bytes=64)
+        k_split = pool.tile([P, PASSES, N], U16, name="k_split", tag="zero", align_bytes=64)
         part_words(k_split, k_pairs, slice(0, N))
         quantise(1)
 

@@ -93,12 +93,13 @@ def tile_attend_questgrp_topk_kernel(tc, qT, k_words, k_scales, c_words, c_scale
         codes = pool.tile([P, PASSES, 2, NQ], U32, name="codes", align_bytes=64)
         scales = pool.tile([P, PASSES, 2, NQ], U8, name="scales", align_bytes=64)
 
-        def part_q(o, last_bias):
+        def positive_part(o, rows, bias):
+            view = q_raw[o][:, :, rows].rearrange("p j n -> p n j")
+            nc.scalar.activation(out=parts[:, o, K_SIDE, rows], in_=view, func=ACT.Relu, bias=bias[:], scale=1.0)
+
+        def negative_part(o):
             view = q_raw[o][:].rearrange("p j n -> p n j")
-            flipped = pool.tile([P, NQ, PACK], BF16, name="flipped%d" % o, align_bytes=64)
-            nc.scalar.activation(out=flipped[:], in_=view, func=ACT.Relu, bias=zero[:], scale=-1.0)
-            nc.scalar.activation(out=parts[:, o, K_SIDE], in_=view, func=ACT.Relu, bias=last_bias[:], scale=1.0)
-            return flipped
+            nc.vector.tensor_scalar(out=parts[:, o, C_SIDE], in0=view, scalar1=0.0, scalar2=None, op0=ALU.min)
 
         def quantise(o):
             nc.vector.quantize_mx(
@@ -113,8 +114,8 @@ def tile_attend_questgrp_topk_kernel(tc, qT, k_words, k_scales, c_words, c_scale
                 in_=pairs[:, cols].bitcast(U16).rearrange("p (n o) -> p o n", o=PASSES),
             )
 
-        flipped = part_q(0, zero)
-        nc.scalar.activation(out=parts[:, 0, C_SIDE], in_=flipped[:], func=ACT.Copy, scale=-1.0)
+        positive_part(0, slice(0, NQ), zero)
+        negative_part(0)
         quantise(0)
 
         k_pairs = pool.tile([P, N], U32, name="k_pairs", align_bytes=64)
@@ -129,8 +130,9 @@ def tile_attend_questgrp_topk_kernel(tc, qT, k_words, k_scales, c_words, c_scale
             start=True,
             stop=True,
         )
-        flipped = part_q(1, blank)
-        nc.vector.tensor_scalar(out=parts[:, 1, C_SIDE], in0=flipped[:], scalar1=-1.0, scalar2=None, op0=ALU.mult)
+        positive_part(1, slice(0, NQ // 2), zero)
+        positive_part(1, slice(NQ // 2, NQ), blank)
+        negative_part(1)
         k_split = pool.tile([P, PASSES, N], U16, name="k_split", tag="zero", align_bytes=64)
         part_words(k_split, k_pairs, slice(0, N))
         quantise(1)

@@ -120,16 +120,6 @@ def tile_attend_questgrp_topk_kernel(tc, qT, k_words, k_scales, c_words, c_scale
 
         k_pairs = pool.tile([P, N], U32, name="k_pairs", align_bytes=64)
         nc.vector.tensor_copy(k_pairs[:], k_pool[:].bitcast(U32).indirect(offsets[:]))
-        spare = psum.tile([P, N], F32, name="spare")
-        nc.tensor.matmul_mx(
-            out=spare[:],
-            lhsT=codes[:, 0, K_SIDE].bitcast(FP8X4),
-            lhsT_scale=scales[:, 0, K_SIDE],
-            rhs=k_pairs[:, 0:HALF].bitcast(U16).bitcast(FP4X4),
-            rhs_scale=picked[:, K_SIDE, :],
-            start=True,
-            stop=True,
-        )
         positive_part(1, slice(0, NQ // 2), zero)
         positive_part(1, slice(NQ // 2, NQ), blank)
         negative_part(1)

@@ -29,13 +29,13 @@ def tile_attend_questgrp_topk_kernel(tc, qT, k_words, k_scales, c_words, c_scale
     nc = tc.nc
     with ExitStack() as ctx:
         pool = ctx.enter_context(tc.tile_pool(name="held", bufs=1))
+        shared = ctx.enter_context(tc.tile_pool(name="shared", bufs=1))
         psum = ctx.enter_context(tc.psum_pool(name="psum", bufs=1))
 
         offsets = pool.tile([P, N // 16], U16, name="offsets")
         nc.sync.dma_start(offsets[:], offs)
 
-        def load_scale_rows(name, scales, row0, empty, clearer):
-            rows = pool.tile([P, T], U8, name=name, tag=name, align_bytes=64)
+        def load_scale_rows(rows, scales, row0, empty, clearer):
             nc.sync.dma_start(
                 out=rows[row0 : row0 + 32, :].bitcast(I32),
                 in_=scales.bitcast(I32).rearrange("o f t -> f o t"),
@@ -45,60 +45,62 @@ def tile_attend_questgrp_topk_kernel(tc, qT, k_words, k_scales, c_words, c_scale
             return rows
 
         row0 = 96
-        k_rows = load_scale_rows("k_rows", k_scales, row0, [(0, 96)], nc.vector)
-        c_rows = load_scale_rows("c_rows", c_scales, row0, [(0, 96)], nc.gpsimd)
+        k_rows = shared.tile([P, T], U8, name="k_rows", align_bytes=64, offset=0)
+        c_rows = pool.tile([P, T], U8, name="c_rows", tag="c_rows", align_bytes=64)
+        load_scale_rows(k_rows, k_scales, row0, [(0, 96)], nc.vector)
+        load_scale_rows(c_rows, c_scales, row0, [(0, 96)], nc.gpsimd)
 
-        def load_q(o, tag):
-            raw = pool.tile([P, PACK, NQ], F32, name="q_raw%d" % o, tag=tag)
-            nc.sync.dma_start(
-                out=raw[:].rearrange("p j n -> p (j n)"),
-                in_=qT[0, o * P * PACK : (o + 1) * P * PACK, :].rearrange("(p j) n -> p (j n)", j=PACK),
-            )
-            return raw
+        q_both = pool.tile([P, PASSES, PACK, NQ], F32, name="q_both")
+        nc.sync.dma_start(
+            out=q_both[:].rearrange("p o j n -> p o (j n)"),
+            in_=qT[0].rearrange("(o p j) n -> p o (j n)", o=PASSES, j=PACK),
+        )
 
-        def load_words(name, words, tag):
-            held = pool.tile([P, T], I32, name=name, tag=tag, align_bytes=64)
+        def load_words(held, words):
             nc.sync.dma_start(out=held[:], in_=words[0].rearrange("p t b -> p (t b)").bitcast(I32))
             return held
 
-        q_raw = [load_q(0, "q_raw0")]
-        k_pool = load_words("k_pool", k_words, "k_pool")
-        q_raw.append(load_q(1, "q_then_th"))
-        c_pool = load_words("c_pool", c_words, "c_pool")
+        k_pool = pool.tile([P, T], I32, name="k_pool", tag="k_pool")
+        load_words(k_pool, k_words)
 
         blank = pool.tile([P, 1], F32, name="blank")
         nc.gpsimd.memset(blank[:], 0.0)
-        zero = pool.tile([P, 1], F32, name="zero", tag="zero", align_bytes=64)
+        zero = pool.tile([P, 1], F32, name="zero")
         nc.scalar.activation(out=zero[:], in_=blank[:], func=ACT.Relu)
 
         picked = pool.tile([P, 2, N], U8, name="picked", align_bytes=64)
         nc.vector.tensor_copy(picked[:, K_SIDE, :], k_rows[:].indirect(offsets[:]))
         nc.vector.tensor_copy(picked[:, C_SIDE, :], c_rows[:].indirect(offsets[:]))
 
-        planes = pool.tile([P, PASSES, 2, N], U8, name="planes", tag="k_rows", align_bytes=64)
+        k_planes = shared.tile([P, PASSES, N], U8, name="k_planes", align_bytes=64, offset=0)
+        c_planes = pool.tile([P, PASSES, N], U8, name="c_planes", tag="c_rows", align_bytes=64)
+        planes = [k_planes, c_planes]
 
-        def spread(quad, sides):
-            nc.sync.dma_start(
-                out=planes[32 * quad : 32 * quad + 4, :, sides, :].rearrange("p o s n -> p o (s n)").bitcast(I32),
-                in_=picked[row0 + 8 * quad : row0 + 8 * quad + 8, sides, :].rearrange("p s n -> p (s n)").bitcast(I32),
+        def spread(queue, quad, side):
+            queue.dma_start(
+                out=planes[side][32 * quad : 32 * quad + 4].bitcast(I32),
+                in_=picked[row0 + 8 * quad : row0 + 8 * quad + 8, side, :].bitcast(I32),
             )
 
-        for quad in (0, 2, 1):
-            spread(quad, slice(K_SIDE, K_SIDE + 1))
-        spread(3, slice(0, 2))
-        for quad in (0, 1, 2):
-            spread(quad, slice(C_SIDE, C_SIDE + 1))
+        for quad in (2, 3):
+            spread(nc.scalar, quad, K_SIDE)
+        c_pool = shared.tile([P, T], I32, name="c_pool", align_bytes=64, offset=PASSES * N)
+        load_words(c_pool, c_words)
+        for quad in (0, 1):
+            spread(nc.sync, quad, K_SIDE)
+        for quad in (2, 0, 3, 1):
+            spread(nc.sync, quad, C_SIDE)
 
         parts = pool.tile([P, PASSES, 2, NQ, PACK], BF16, name="parts", align_bytes=64)
         codes = pool.tile([P, PASSES, 2, NQ], U32, name="codes", align_bytes=64)
         scales = pool.tile([P, PASSES, 2, NQ], U8, name="scales", align_bytes=64)
 
-        def positive_part(o, rows, bias):
-            view = q_raw[o][:, :, rows].rearrange("p j n -> p n j")
-            nc.scalar.activation(out=parts[:, o, K_SIDE, rows], in_=view, func=ACT.Relu, bias=bias[:], scale=1.0)
+        def positive_part(o):
+            view = q_both[:, o].rearrange("p j n -> p n j")
+            nc.scalar.activation(out=parts[:, o, K_SIDE], in_=view, func=ACT.Relu, bias=zero[:], scale=1.0)
 
         def negative_part(o):
-            view = q_raw[o][:].rearrange("p j n -> p n j")
+            view = q_both[:, o].rearrange("p j n -> p n j")
             nc.vector.tensor_scalar(out=parts[:, o, C_SIDE], in0=view, scalar1=0.0, scalar2=None, op0=ALU.min)
 
         def quantise(o):
@@ -114,20 +116,18 @@ def tile_attend_questgrp_topk_kernel(tc, qT, k_words, k_scales, c_words, c_scale
                 in_=pairs[:, cols].bitcast(U16).rearrange("p (n o) -> p o n", o=PASSES),
             )
 
-        positive_part(0, slice(0, NQ), zero)
-        negative_part(0)
-        quantise(0)
+        for o in range(PASSES):
+            positive_part(o)
+            negative_part(o)
+        for o in range(PASSES):
+            quantise(o)
 
         k_pairs = pool.tile([P, N], U32, name="k_pairs", align_bytes=64)
         nc.vector.tensor_copy(k_pairs[:], k_pool[:].bitcast(U32).indirect(offsets[:]))
-        positive_part(1, slice(0, NQ // 2), zero)
-        positive_part(1, slice(NQ // 2, NQ), blank)
-        negative_part(1)
-        k_split = pool.tile([P, PASSES, N], U16, name="k_split", tag="zero", align_bytes=64)
+        k_split = pool.tile([P, PASSES, N], U16, name="k_split", align_bytes=64)
         part_words(k_split, k_pairs, slice(0, N))
-        quantise(1)
 
-        th_sb = pool.tile([P, 1], F32, name="th_sb", tag="q_then_th")
+        th_sb = pool.tile([P, 1], F32, name="th_sb", tag="k_pool")
         nc.sync.dma_start(out=th_sb[:], in_=th[0])
 
         banks = [psum.tile([P, GROUP], F32, name="bank%d" % g) for g in range(GROUPS)]
@@ -139,7 +139,7 @@ def tile_attend_questgrp_topk_kernel(tc, qT, k_words, k_scales, c_words, c_scale
                 lhsT=codes[:, o, side].bitcast(FP8X4),
                 lhsT_scale=scales[:, o, side],
                 rhs=words[:, o, cols].bitcast(FP4X4),
-                rhs_scale=planes[:, o, side, cols],
+                rhs_scale=planes[side][:, o, cols],
                 start=(side == K_SIDE and o == 0),
                 stop=(side == C_SIDE and o == PASSES - 1),
             )

@@ -50,18 +50,18 @@ def tile_attend_questgrp_topk_kernel(tc, qT, k_words, k_scales, c_words, c_scale
         load_scale_rows(k_rows, k_scales, row0, [(0, 96)], nc.vector)
         load_scale_rows(c_rows, c_scales, row0, [(0, 96)], nc.gpsimd)
 
-        q_both = pool.tile([P, PASSES, PACK, NQ], F32, name="q_both")
-        nc.sync.dma_start(
-            out=q_both[:].rearrange("p o j n -> p o (j n)"),
-            in_=qT[0].rearrange("(o p j) n -> p o (j n)", o=PASSES, j=PACK),
-        )
-
         def load_words(held, words):
             nc.sync.dma_start(out=held[:], in_=words[0].rearrange("p t b -> p (t b)").bitcast(I32))
             return held
 
         k_pool = pool.tile([P, T], I32, name="k_pool", tag="k_pool")
         load_words(k_pool, k_words)
+        q_both = pool.tile([P, PASSES, PACK, NQ], F32, name="q_both")
+        nc.sync.dma_start(
+            out=q_both[:].rearrange("p o j n -> p o (j n)"),
+            in_=qT[0].rearrange("(o p j) n -> p o (j n)", o=PASSES, j=PACK),
+        )
+
 
         blank = pool.tile([P, 1], F32, name="blank")
         nc.gpsimd.memset(blank[:], 0.0)
@@ -82,12 +82,10 @@ def tile_attend_questgrp_topk_kernel(tc, qT, k_words, k_scales, c_words, c_scale
                 in_=picked[row0 + 8 * quad : row0 + 8 * quad + 8, side, :].bitcast(I32),
             )
 
-        for quad in (2, 3):
+        for quad in (0, 2, 1, 3):
             spread(nc.scalar, quad, K_SIDE)
         c_pool = shared.tile([P, T], I32, name="c_pool", align_bytes=64, offset=PASSES * N)
         load_words(c_pool, c_words)
-        for quad in (0, 1):
-            spread(nc.sync, quad, K_SIDE)
         for quad in (2, 0, 3, 1):
             spread(nc.sync, quad, C_SIDE)
 
@@ -116,16 +114,21 @@ def tile_attend_questgrp_topk_kernel(tc, qT, k_words, k_scales, c_words, c_scale
                 in_=pairs[:, cols].bitcast(U16).rearrange("p (n o) -> p o n", o=PASSES),
             )
 
+        k_pairs = pool.tile([P, N], U32, name="k_pairs", align_bytes=64)
+        for h in range(2):
+            nc.vector.tensor_copy(
+                k_pairs[:, h * HALF : (h + 1) * HALF],
+                k_pool[:].bitcast(U32).indirect(offsets[:, h * HALF // 16 : (h + 1) * HALF // 16]),
+            )
+        k_split = pool.tile([P, PASSES, N], U16, name="k_split", align_bytes=64)
+        for h in range(2):
+            part_words(k_split, k_pairs, slice(h * HALF, (h + 1) * HALF))
+
         for o in range(PASSES):
             positive_part(o)
             negative_part(o)
         for o in range(PASSES):
             quantise(o)
-
-        k_pairs = pool.tile([P, N], U32, name="k_pairs", align_bytes=64)
-        nc.vector.tensor_copy(k_pairs[:], k_pool[:].bitcast(U32).indirect(offsets[:]))
-        k_split = pool.tile([P, PASSES, N], U16, name="k_split", align_bytes=64)
-        part_words(k_split, k_pairs, slice(0, N))
 
         th_sb = pool.tile([P, 1], F32, name="th_sb", tag="k_pool")
         nc.sync.dma_start(out=th_sb[:], in_=th[0])

@@ -23,71 +23,65 @@ GROUP = 128
 GROUPS = N // GROUP
 HALF = N // 2
 K_SIDE, C_SIDE = 0, 1
+ROWS = 32
 
 
 def tile_attend_questgrp_topk_kernel(tc, qT, k_words, k_scales, c_words, c_scales, th, offs, out):
     nc = tc.nc
     with ExitStack() as ctx:
         pool = ctx.enter_context(tc.tile_pool(name="held", bufs=1))
-        shared = ctx.enter_context(tc.tile_pool(name="shared", bufs=1))
         psum = ctx.enter_context(tc.psum_pool(name="psum", bufs=1))
 
         offsets = pool.tile([P, N // 16], U16, name="offsets")
         nc.sync.dma_start(offsets[:], offs)
 
-        def load_scale_rows(rows, scales, row0, empty, clearer):
+        first_row = (96, 32)
+        row_step = (1, 2)
+
+        def scale_rows(tile, side, start, count):
+            a = first_row[side] + row_step[side] * start
+            return tile[a : a + row_step[side] * count : row_step[side]]
+
+        def load_scale_rows(rows, side, scales):
             nc.sync.dma_start(
-                out=rows[row0 : row0 + 32, :].bitcast(I32),
+                out=scale_rows(rows, side, 0, ROWS).bitcast(I32),
                 in_=scales.bitcast(I32).rearrange("o f t -> f o t"),
             )
-            for a, b in empty:
-                clearer.memset(rows[a:b, :].bitcast(I32), 0)
-            return rows
 
-        row0 = 96
-        k_rows = shared.tile([P, T], U8, name="k_rows", align_bytes=64, offset=0)
+        k_rows = pool.tile([P, T], U8, name="k_rows", tag="k_rows", align_bytes=64)
         c_rows = pool.tile([P, T], U8, name="c_rows", tag="c_rows", align_bytes=64)
-        load_scale_rows(k_rows, k_scales, row0, [(0, 96)], nc.vector)
-        load_scale_rows(c_rows, c_scales, row0, [(0, 96)], nc.gpsimd)
+        nc.vector.memset(c_rows[:].bitcast(I32), 0)
+        load_scale_rows(k_rows, K_SIDE, k_scales)
+        nc.vector.memset(k_rows[: first_row[K_SIDE]].bitcast(I32), 0)
 
-        def load_words(held, words):
-            nc.sync.dma_start(out=held[:], in_=words[0].rearrange("p t b -> p (t b)").bitcast(I32))
-            return held
-
-        k_pool = pool.tile([P, T], I32, name="k_pool", tag="k_pool")
-        load_words(k_pool, k_words)
         q_both = pool.tile([P, PASSES, PACK, NQ], F32, name="q_both")
         nc.sync.dma_start(
             out=q_both[:].rearrange("p o j n -> p o (j n)"),
             in_=qT[0].rearrange("(o p j) n -> p o (j n)", o=PASSES, j=PACK),
         )
+        load_scale_rows(c_rows, C_SIDE, c_scales)
 
+        def load_words(held, words):
+            nc.sync.dma_start(out=held[:], in_=words[0].rearrange("p t b -> p (t b)").bitcast(I32))
 
-        blank = pool.tile([P, 1], F32, name="blank")
-        nc.gpsimd.memset(blank[:], 0.0)
-        zero = pool.tile([P, 1], F32, name="zero")
-        nc.scalar.activation(out=zero[:], in_=blank[:], func=ACT.Relu)
+        k_pool = pool.tile([P, T], I32, name="k_pool", tag="k_pool")
+        load_words(k_pool, k_words)
+        c_pool = pool.tile([P, T], I32, name="c_pool")
+        load_words(c_pool, c_words)
 
         picked = pool.tile([P, 2, N], U8, name="picked", align_bytes=64)
         nc.vector.tensor_copy(picked[:, K_SIDE, :], k_rows[:].indirect(offsets[:]))
         nc.vector.tensor_copy(picked[:, C_SIDE, :], c_rows[:].indirect(offsets[:]))
 
-        k_planes = shared.tile([P, PASSES, N], U8, name="k_planes", align_bytes=64, offset=0)
+        k_planes = pool.tile([P, PASSES, N], U8, name="k_planes", tag="k_rows", align_bytes=64)
         c_planes = pool.tile([P, PASSES, N], U8, name="c_planes", tag="c_rows", align_bytes=64)
         planes = [k_planes, c_planes]
-
-        def spread(queue, quad, side):
-            queue.dma_start(
-                out=planes[side][32 * quad : 32 * quad + 4].bitcast(I32),
-                in_=picked[row0 + 8 * quad : row0 + 8 * quad + 8, side, :].bitcast(I32),
-            )
-
-        for quad in (0, 2, 1, 3):
-            spread(nc.scalar, quad, K_SIDE)
-        c_pool = shared.tile([P, T], I32, name="c_pool", align_bytes=64, offset=PASSES * N)
-        load_words(c_pool, c_words)
-        for quad in (2, 0, 3, 1):
-            spread(nc.sync, quad, C_SIDE)
+        for side in (K_SIDE, C_SIDE):
+            for quad in (0, 2, 1, 3):
+                nc.sync.dma_start(
+                    out=planes[side][32 * quad : 32 * quad + 4].bitcast(I32),
+                    in_=scale_rows(picked, side, 8 * quad, 8)[:, side, :].bitcast(I32),
+                )
 
         parts = pool.tile([P, PASSES, 2, NQ, PACK], BF16, name="parts", align_bytes=64)
         codes = pool.tile([P, PASSES, 2, NQ], U32, name="codes", align_bytes=64)
@@ -95,7 +89,7 @@ def tile_attend_questgrp_topk_kernel(tc, qT, k_words, k_scales, c_words, c_scale
 
         def positive_part(o):
             view = q_both[:, o].rearrange("p j n -> p n j")
-            nc.scalar.activation(out=parts[:, o, K_SIDE], in_=view, func=ACT.Relu, bias=zero[:], scale=1.0)
+            nc.scalar.activation(out=parts[:, o, K_SIDE], in_=view, func=ACT.Relu)
 
         def negative_part(o):
             view = q_both[:, o].rearrange("p j n -> p n j")
@@ -107,6 +101,12 @@ def tile_attend_questgrp_topk_kernel(tc, qT, k_words, k_scales, c_words, c_scale
                 scales=scales[:, o].rearrange("p s n -> p (s n)"),
                 in_=parts[:, o].rearrange("p s n j -> p (s n j)"),
             )
+
+        for o in range(PASSES):
+            positive_part(o)
+            negative_part(o)
+        for o in range(PASSES):
+            quantise(o)
 
         def part_words(words, pairs, cols):
             nc.vector.tensor_copy(
@@ -123,12 +123,6 @@ def tile_attend_questgrp_topk_kernel(tc, qT, k_words, k_scales, c_words, c_scale
         k_split = pool.tile([P, PASSES, N], U16, name="k_split", align_bytes=64)
         for h in range(2):
             part_words(k_split, k_pairs, slice(h * HALF, (h + 1) * HALF))
-
-        for o in range(PASSES):
-            positive_part(o)
-            negative_part(o)
-        for o in range(PASSES):
-            quantise(o)
 
         th_sb = pool.tile([P, 1], F32, name="th_sb", tag="k_pool")
         nc.sync.dma_start(out=th_sb[:], in_=th[0])

@@ -141,6 +141,18 @@ def tile_attend_questgrp_topk_kernel(tc, qT, k_words, k_scales, c_words, c_scale
                 stop=(side == C_SIDE and o == PASSES - 1),
             )
 
+        spare = psum.tile([P, 2, GROUP], F32, name="spare")
+        for slot, width in enumerate((GROUP, GROUP // 2)):
+            nc.tensor.matmul_mx(
+                out=spare[:, slot, :width],
+                lhsT=codes[:, 0, K_SIDE].bitcast(FP8X4),
+                lhsT_scale=scales[:, 0, K_SIDE],
+                rhs=k_split[:, slot, N - width :].bitcast(FP4X4),
+                rhs_scale=scales[:, 0, K_SIDE, :width],
+                start=True,
+                stop=True,
+            )
+
         for o in range(PASSES):
             for g in range(GROUPS):
                 multiply(g, o, k_split, K_SIDE)

from contextlib import ExitStack

import concourse.mybir as mybir

N, T, D, NQ, SEG = 512, 2048, 1024, 128, 8
FLOPS = 2 * 2 * NQ * N * D

F32 = mybir.dt.float32
BF16 = mybir.dt.bfloat16
I32 = mybir.dt.int32
U32 = mybir.dt.uint32
U16 = mybir.dt.uint16
U8 = mybir.dt.uint8
FP8X4 = mybir.dt.float8_e4m3fn_x4
FP4X4 = mybir.dt.float4_e2m1fn_x4
ACT = mybir.ActivationFunctionType
ALU = mybir.AluOpType

P = 128
PACK = 4
PASSES = D // (P * PACK)
GROUP = 128
GROUPS = N // GROUP
HALF = N // 2
K_SIDE, C_SIDE = 0, 1
ROWS = 32


def tile_attend_questgrp_topk_kernel(tc, qT, k_words, k_scales, c_words, c_scales, th, offs, out):
    nc = tc.nc
    with ExitStack() as ctx:
        pool = ctx.enter_context(tc.tile_pool(name="held", bufs=1))
        psum = ctx.enter_context(tc.psum_pool(name="psum", bufs=1))

        offsets = pool.tile([P, N // 16], U16, name="offsets")
        nc.sync.dma_start(offsets[:], offs)

        first_row = (96, 32)
        row_step = (1, 2)

        def scale_rows(tile, side, start, count):
            a = first_row[side] + row_step[side] * start
            return tile[a : a + row_step[side] * count : row_step[side]]

        def load_scale_rows(rows, side, scales):
            nc.sync.dma_start(
                out=scale_rows(rows, side, 0, ROWS).bitcast(I32),
                in_=scales.bitcast(I32).rearrange("o f t -> f o t"),
            )

        k_rows = pool.tile([P, T], U8, name="k_rows", tag="k_rows", align_bytes=64)
        c_rows = pool.tile([P, T], U8, name="c_rows", tag="c_rows", align_bytes=64)
        nc.vector.memset(c_rows[:].bitcast(I32), 0)
        load_scale_rows(k_rows, K_SIDE, k_scales)
        nc.vector.memset(k_rows[: first_row[K_SIDE]].bitcast(I32), 0)

        q_both = pool.tile([P, PASSES, PACK, NQ], F32, name="q_both")
        nc.sync.dma_start(
            out=q_both[:].rearrange("p o j n -> p o (j n)"),
            in_=qT[0].rearrange("(o p j) n -> p o (j n)", o=PASSES, j=PACK),
        )
        load_scale_rows(c_rows, C_SIDE, c_scales)

        def load_words(held, words):
            nc.sync.dma_start(out=held[:], in_=words[0].rearrange("p t b -> p (t b)").bitcast(I32))

        k_pool = pool.tile([P, T], I32, name="k_pool", tag="k_pool")
        load_words(k_pool, k_words)
        c_pool = pool.tile([P, T], I32, name="c_pool")
        load_words(c_pool, c_words)

        picked = pool.tile([P, 2, N], U8, name="picked", align_bytes=64)
        nc.vector.tensor_copy(picked[:, K_SIDE, :], k_rows[:].indirect(offsets[:]))
        nc.vector.tensor_copy(picked[:, C_SIDE, :], c_rows[:].indirect(offsets[:]))

        k_planes = pool.tile([P, PASSES, N], U8, name="k_planes", tag="k_rows", align_bytes=64)
        c_planes = pool.tile([P, PASSES, N], U8, name="c_planes", tag="c_rows", align_bytes=64)
        planes = [k_planes, c_planes]
        for side in (K_SIDE, C_SIDE):
            for quad in (0, 2, 1, 3):
                nc.sync.dma_start(
                    out=planes[side][32 * quad : 32 * quad + 4].bitcast(I32),
                    in_=scale_rows(picked, side, 8 * quad, 8)[:, side, :].bitcast(I32),
                )

        parts = pool.tile([P, PASSES, 2, NQ, PACK], BF16, name="parts", align_bytes=64)
        codes = pool.tile([P, PASSES, 2, NQ], U32, name="codes", align_bytes=64)
        scales = pool.tile([P, PASSES, 2, NQ], U8, name="scales", align_bytes=64)

        def positive_part(o):
            view = q_both[:, o].rearrange("p j n -> p n j")
            nc.scalar.activation(out=parts[:, o, K_SIDE], in_=view, func=ACT.Relu)

        def negative_part(o):
            view = q_both[:, o].rearrange("p j n -> p n j")
            nc.vector.tensor_scalar(out=parts[:, o, C_SIDE], in0=view, scalar1=0.0, scalar2=None, op0=ALU.min)

        def quantise(o):
            nc.vector.quantize_mx(
                out=codes[:, o].rearrange("p s n -> p (s n)").bitcast(FP8X4),
                scales=scales[:, o].rearrange("p s n -> p (s n)"),
                in_=parts[:, o].rearrange("p s n j -> p (s n j)"),
            )

        for o in range(PASSES):
            positive_part(o)
            negative_part(o)
        for o in range(PASSES):
            quantise(o)

        def part_words(words, pairs, cols):
            nc.vector.tensor_copy(
                out=words[:, :, cols],
                in_=pairs[:, cols].bitcast(U16).rearrange("p (n o) -> p o n", o=PASSES),
            )

        k_pairs = pool.tile([P, N], U32, name="k_pairs", align_bytes=64)
        for h in range(2):
            nc.vector.tensor_copy(
                k_pairs[:, h * HALF : (h + 1) * HALF],
                k_pool[:].bitcast(U32).indirect(offsets[:, h * HALF // 16 : (h + 1) * HALF // 16]),
            )
        k_split = pool.tile([P, PASSES, N], U16, name="k_split", align_bytes=64)
        for h in range(2):
            part_words(k_split, k_pairs, slice(h * HALF, (h + 1) * HALF))

        th_sb = pool.tile([P, 1], F32, name="th_sb", tag="k_pool")
        nc.sync.dma_start(out=th_sb[:], in_=th[0])

        banks = [psum.tile([P, GROUP], F32, name="bank%d" % g) for g in range(GROUPS)]

        def multiply(g, o, words, side):
            cols = slice(g * GROUP, (g + 1) * GROUP)
            nc.tensor.matmul_mx(
                out=banks[g][:],
                lhsT=codes[:, o, side].bitcast(FP8X4),
                lhsT_scale=scales[:, o, side],
                rhs=words[:, o, cols].bitcast(FP4X4),
                rhs_scale=planes[side][:, o, cols],
                start=(side == K_SIDE and o == 0),
                stop=(side == C_SIDE and o == PASSES - 1),
            )

        spare = psum.tile([P, 2, GROUP], F32, name="spare")
        for slot, width in enumerate((GROUP, GROUP // 2)):
            nc.tensor.matmul_mx(
                out=spare[:, slot, :width],
                lhsT=codes[:, 0, K_SIDE].bitcast(FP8X4),
                lhsT_scale=scales[:, 0, K_SIDE],
                rhs=k_split[:, slot, N - width :].bitcast(FP4X4),
                rhs_scale=scales[:, 0, K_SIDE, :width],
                start=True,
                stop=True,
            )

        for o in range(PASSES):
            for g in range(GROUPS):
                multiply(g, o, k_split, K_SIDE)

        c_pairs = pool.tile([P, N], U32, name="c_pairs", align_bytes=64)
        for h in range(2):
            nc.vector.tensor_copy(
                c_pairs[:, h * HALF : (h + 1) * HALF],
                c_pool[:].bitcast(U32).indirect(offsets[:, h * HALF // 16 : (h + 1) * HALF // 16]),
            )
        c_split = pool.tile([P, PASSES, N], U16, name="c_split", align_bytes=64)
        for g in range(GROUPS):
            part_words(c_split, c_pairs, slice(g * GROUP, (g + 1) * GROUP))
            for o in range(PASSES):
                multiply(g, o, c_split, C_SIDE)

        best = pool.tile([P, N // SEG], F32, name="best")
        runs = GROUP // SEG
        for g in range(GROUPS):
            nc.vector.tensor_reduce(
                out=best[:, g * runs : (g + 1) * runs],
                in_=banks[g][:].rearrange("p (j s) -> p j s", s=SEG),
                axis=mybir.AxisListType.X,
                op=ALU.max,
            )
        result = pool.tile([P, N // SEG], F32, name="result")
        nc.vector.tensor_scalar(out=result[:], in0=best[:], scalar1=th_sb[:], scalar2=None, op0=ALU.subtract)
        nc.sync.dma_start(out=out[0], in_=result[:])
